import numpy as np
import ml_dtypes


def mxq(x, axis, fmt="e4m3"):
    dtype, down = {"e4m3": (ml_dtypes.float8_e4m3fn, 7), "e5m2": (ml_dtypes.float8_e5m2, 14)}[fmt]
    v = np.moveaxis(np.asarray(x, np.float32).astype(ml_dtypes.bfloat16).astype(np.float64), axis, -1)
    blocks = v.reshape(v.shape[:-1] + (-1, 32))
    amax = np.abs(blocks).max(-1, keepdims=True)
    byte = np.maximum(np.where(amax > 0, np.frexp(amax)[1] - 1 + 127, 0) - down, 1)
    scale = np.exp2(byte - 127.0)
    codes = (blocks / scale).astype(np.float32).astype(dtype).astype(np.float64)
    return np.moveaxis((codes * scale).reshape(v.shape), -1, axis)


WIDE = False


def mx_kscale(k):
    if not WIDE:
        return np.ones(k)
    levels = np.array([10, -10, 5, -5, 0])
    if k % 512:
        return np.exp2(np.random.permutation(np.resize(levels, k // 32))).repeat(32)
    a = np.empty((k // 512, 16))
    for p in range(k // 512):
        a[p, :8] = np.random.permutation(np.resize(levels, 8))
        for g in range(8):
            far = levels[np.abs(levels - a[p, g]) >= 10]
            a[p, g + 8] = far[np.random.randint(len(far))]
    return np.exp2(a.ravel()).repeat(32)


def f64(x):
    return np.asarray(x).astype(np.float64)


def striped(idx):
    return np.tile(np.asarray(idx).reshape(-1, 16).T, (8, 1)).astype(np.uint16)


def unstriped(offs):
    return offs[:16].T.reshape(-1).astype(np.int64)


D, T, I, Q, E = 512, 2048, 512, 128, 512


def setup_inputs():
    n = np.random.standard_normal
    idx = np.random.permutation(T)[:I]
    idx2 = np.random.permutation(T)[:I]
    idx3 = np.random.permutation(T)[:I]
    fd = mx_kscale(D)
    fi = mx_kscale(I)
    ti = np.ones(T)
    ti[idx] = fi
    return {
        "query": (n((D, Q)) * 1.0 / np.sqrt(D) * fd[:, None]).astype(np.float32),
        "keys": (n((D, T)) / fd[:, None]).astype(np.float32),
        "os": (np.random.uniform(0.02, 0.08, (1, I)) * fi).astype(np.float32),
        "vals": (n((E, T)) / ti).astype(np.float32),
        "offs": striped(idx),
        "offs2": striped(idx2),
        "offs3": striped(idx3),
    }


def reference(query, keys, os, vals, offs, offs2, offs3):
    idx = unstriped(offs)
    idx2 = unstriped(offs2)
    idx3 = unstriped(offs3)
    lo3 = np.minimum(f64(keys)[:, idx], f64(keys)[:, idx2])
    hi3 = np.maximum(f64(keys)[:, idx], f64(keys)[:, idx2])
    zk = np.maximum(lo3, np.minimum(hi3, f64(keys)[:, idx3]))
    queryq = mxq(f64(query), 0, "e4m3")
    zkq = mxq(zk, 0, "e4m3")
    s = queryq.T @ zkq
    w = np.maximum(s, 0.0)
    wo1 = w * f64(os)
    wt1 = wo1.T
    vt1 = f64(vals)[:, idx].T
    wt1q = mxq(wt1, 0, "e4m3")
    vt1q = mxq(vt1, 0, "e4m3")
    o = wt1q.T @ vt1q
    return o

@@ -1,0 +1,135 @@
+from contextlib import ExitStack
+
+import concourse.mybir as mybir
+from concourse.masks import make_identity
+
+D, T, I, Q, E = 512, 2048, 512, 128, 512
+FLOPS = 2 * Q * I * D + 2 * Q * E * I
+
+F32 = mybir.dt.float32
+BF16 = mybir.dt.bfloat16
+U32 = mybir.dt.uint32
+U16 = mybir.dt.uint16
+U8 = mybir.dt.uint8
+FP8X4 = mybir.dt.float8_e4m3fn_x4
+ALU = mybir.AluOpType
+COPY = mybir.ActivationFunctionType.Copy
+
+P = 128
+PACK = 4
+
+
+def tile_attend_keymiddle_read_lean_kernel(tc, query, keys, slot_factor, vals, offs, offs2, offs3, out):
+    nc = tc.nc
+    with ExitStack() as ctx:
+        held = ctx.enter_context(tc.tile_pool(name="held", bufs=1))
+        psum = ctx.enter_context(tc.psum_pool(name="psum", bufs=1))
+
+        lists = [held.tile([P, I // 16], U16, name=f"list{n}") for n in range(3)]
+        key_pool = [held.tile([P, T], F32, name=f"key_pool{t}") for t in range(PACK)]
+        val_pool = [held.tile([P, T], F32, name=f"val_pool{g}", align_bytes=64) for g in range(E // P)]
+        q_raw = held.tile([P, PACK, Q], F32, name="q_raw")
+        factor = held.tile([P, PACK], F32, name="factor")
+        ident = held.tile([P, P], F32, name="ident")
+
+        keys_by_place = keys.rearrange("(p t) c -> p t c", t=PACK)
+        nc.sync.dma_start(q_raw[:], query.rearrange("(p t) q -> p t q", t=PACK))
+        nc.sync.dma_start(key_pool[0][:], keys_by_place[:, 0, :])
+        for tile, src in zip(lists, (offs, offs2, offs3)):
+            nc.sync.dma_start(tile[:], src)
+        for t in range(1, PACK):
+            nc.sync.dma_start(key_pool[t][:], keys_by_place[:, t, :])
+        nc.sync.dma_start(factor[:], slot_factor.rearrange("o (p r) -> (o p) r", r=PACK))
+        for g in range(E // P):
+            nc.sync.dma_start(val_pool[g][:], vals[g * P : (g + 1) * P, :])
+        make_identity(nc, ident[:])
+
+        def on_vector(dst, window, offsets):
+            nc.vector.tensor_copy(dst, window[:].indirect(offsets))
+
+        def on_scalar(dst, window, offsets):
+            nc.scalar.activation(dst, window[:].indirect(offsets), COPY)
+
+        q_bf = held.tile([P, Q, PACK], BF16, name="q_bf", align_bytes=64)
+        q_codes = held.tile([P, Q], U32, name="q_codes", align_bytes=64)
+        q_scales = held.tile([P, Q], U8, name="q_scales", align_bytes=64)
+        nc.scalar.activation(q_bf[:], q_raw[:].rearrange("p t q -> p q t"), COPY)
+        nc.vector.quantize_mx(q_codes[:].bitcast(FP8X4), q_scales[:], q_bf[:].rearrange("p q t -> p (q t)"))
+
+        lo = held.tile([P, PACK, I], F32, name="lo")
+        capped = held.tile([P, PACK, I], F32, name="capped")
+        for t in range(PACK):
+            first = held.tile([P, I], F32, name=f"first{t}")
+            second = held.tile([P, I], F32, name=f"second{t}")
+            third = held.tile([P, I], F32, name=f"third{t}")
+            hi = held.tile([P, I], F32, name=f"hi{t}")
+            on_scalar(first[:], key_pool[t], lists[0][:])
+            on_vector(second[:], key_pool[t], lists[1][:])
+            on_scalar(third[:], key_pool[t], lists[2][:])
+            nc.vector.tensor_tensor(hi[:], first[:], second[:], ALU.max)
+            nc.vector.tensor_tensor(lo[:, t, :], first[:], second[:], ALU.min)
+            nc.vector.tensor_tensor(capped[:, t, :], hi[:], third[:], ALU.min)
+
+        zk_bf = held.tile([P, PACK, P, PACK], BF16, name="zk_bf", align_bytes=64)
+        nc.vector.tensor_tensor(
+            zk_bf[:].rearrange("p r s t -> p s t r"),
+            lo[:].rearrange("p t (s r) -> p s t r", r=PACK),
+            capped[:].rearrange("p t (s r) -> p s t r", r=PACK),
+            ALU.max,
+        )
+        zk_codes = held.tile([P, I], U32, name="zk_codes", align_bytes=64)
+        zk_scales = held.tile([P, I], U8, name="zk_scales", align_bytes=64)
+        nc.vector.quantize_mx(zk_codes[:].bitcast(FP8X4), zk_scales[:], zk_bf[:].rearrange("p r s t -> p (r s t)"))
+
+        turned = []
+
+        def pick_and_turn(g):
+            picked = held.tile([P, I], BF16, name=f"picked{g}")
+            on_scalar(picked[:], val_pool[g], lists[0][:])
+            words = picked[:].bitcast(F32)
+            bank = psum.tile([P, 2, P], F32, name=f"turned{g}")
+            for u in range(2):
+                nc.tensor.transpose(bank[:, u, :], words[:, u : I // 2 : 2], ident[:])
+            turned.append(bank)
+
+        v_codes = held.tile([P, E], U32, name="v_codes", align_bytes=64)
+        v_scales = held.tile([P, E], U8, name="v_scales", align_bytes=64)
+
+        def weave_and_quantize(g, tag):
+            cols = slice(g * P, (g + 1) * P)
+            v_bf = held.tile([P, P * PACK], BF16, name=f"v_bf{g}", tag=tag, align_bytes=64)
+            nc.scalar.copy(v_bf[:].bitcast(F32).rearrange("p (e u) -> p e u", u=2), turned[g][:].rearrange("p u e -> p e u"))
+            nc.vector.quantize_mx(v_codes[:, cols].bitcast(FP8X4), v_scales[:, cols], v_bf[:])
+
+        pick_and_turn(0)
+        pick_and_turn(1)
+        weave_and_quantize(0, "val_pool1")
+        pick_and_turn(2)
+        weave_and_quantize(1, "val_pool2")
+
+        scores = psum.tile([P, PACK, Q], F32, name="scores", tag="turned1")
+        for r in range(PACK):
+            cols = slice(r * P, (r + 1) * P)
+            nc.tensor.matmul_mx(scores[:, r, :], zk_codes[:, cols].bitcast(FP8X4), zk_scales[:, cols],
+                                q_codes[:].bitcast(FP8X4), q_scales[:], start=True, stop=True)
+        w_bf = held.tile([P, Q, PACK], BF16, name="w_bf", align_bytes=64)
+        nc.vector.scalar_tensor_tensor(
+            w_bf[:], scores[:].rearrange("p r q -> p q r"), 0.0,
+            factor[:].unsqueeze(1).to_broadcast([P, Q, PACK]), ALU.max, ALU.mult)
+        w_codes = held.tile([P, Q], U32, name="w_codes", align_bytes=64)
+        w_scales = held.tile([P, Q], U8, name="w_scales", align_bytes=64)
+        nc.vector.quantize_mx(w_codes[:].bitcast(FP8X4), w_scales[:], w_bf[:].rearrange("p q r -> p (q r)"))
+
+        weave_and_quantize(2, "v_bf2")
+        pick_and_turn(3)
+        weave_and_quantize(3, "v_bf3")
+
+        early = psum.tile([P, 3 * P], F32, name="early")
+        late = psum.tile([P, P], F32, name="late")
+        for acc, cols in ((early[:, 0 : 2 * P], slice(0, 2 * P)), (early[:, 2 * P : 3 * P], slice(2 * P, 3 * P)), (late[:], slice(3 * P, E))):
+            nc.tensor.matmul_mx(acc, w_codes[:].bitcast(FP8X4), w_scales[:],
+                                v_codes[:, cols].bitcast(FP8X4), v_scales[:, cols], start=True, stop=True)
+        for bank, cols in ((early, slice(0, 3 * P)), (late, slice(3 * P, E))):
+            result = held.tile([P, cols.stop - cols.start], F32, name=f"result{cols.start}")
+            nc.vector.tensor_copy(result[:], bank[:])
+            nc.sync.dma_start(out[:, cols], result[:])

@@ -17,6 +17,8 @@ COPY = mybir.ActivationFunctionType.Copy
 
 P = 128
 PACK = 4
+LAST_THIRD_ON_VECTOR = 256
+LAST_VALUES_ON_VECTOR = 256
 
 
 def tile_attend_keymiddle_read_lean_kernel(tc, query, keys, slot_factor, vals, offs, offs2, offs3, out):
@@ -64,8 +66,12 @@ def tile_attend_keymiddle_read_lean_kernel(tc, query, keys, slot_factor, vals, o
             third = held.tile([P, I], F32, name=f"third{t}")
             hi = held.tile([P, I], F32, name=f"hi{t}")
             on_scalar(first[:], key_pool[t], lists[0][:])
-            on_vector(second[:], key_pool[t], lists[1][:])
-            on_scalar(third[:], key_pool[t], lists[2][:])
+            (on_vector if t < 2 else on_scalar)(second[:], key_pool[t], lists[1][:])
+            shared = (0, 0, I, LAST_THIRD_ON_VECTOR)[t]
+            if shared > 0:
+                on_vector(third[:, 0:shared], key_pool[t], lists[2][:, 0 : shared // 16])
+            if shared < I:
+                on_scalar(third[:, shared:I], key_pool[t], lists[2][:, shared // 16 : I // 16])
             nc.vector.tensor_tensor(hi[:], first[:], second[:], ALU.max)
             nc.vector.tensor_tensor(lo[:, t, :], first[:], second[:], ALU.min)
             nc.vector.tensor_tensor(capped[:, t, :], hi[:], third[:], ALU.min)
@@ -84,52 +90,64 @@ def tile_attend_keymiddle_read_lean_kernel(tc, query, keys, slot_factor, vals, o
         turned = []
 
         def pick_and_turn(g):
-            picked = held.tile([P, I], BF16, name=f"picked{g}")
-            on_scalar(picked[:], val_pool[g], lists[0][:])
+            picked = held.tile([P, I], BF16, name=f"picked{g}", align_bytes=64)
+            shared = LAST_VALUES_ON_VECTOR if g == E // P - 1 else 0
+            if shared:
+                on_vector(picked[:, 0:shared], val_pool[g], lists[0][:, 0 : shared // 16])
+            on_scalar(picked[:, shared:I], val_pool[g], lists[0][:, shared // 16 : I // 16])
             words = picked[:].bitcast(F32)
             bank = psum.tile([P, 2, P], F32, name=f"turned{g}")
             for u in range(2):
                 nc.tensor.transpose(bank[:, u, :], words[:, u : I // 2 : 2], ident[:])
             turned.append(bank)
 
-        v_codes = held.tile([P, E], U32, name="v_codes", align_bytes=64)
-        v_scales = held.tile([P, E], U8, name="v_scales", align_bytes=64)
+        def weave(g, dst):
+            nc.scalar.copy(dst.bitcast(F32).rearrange("p (e u) -> p e u", u=2), turned[g][:].rearrange("p u e -> p e u"))
 
-        def weave_and_quantize(g, tag):
-            cols = slice(g * P, (g + 1) * P)
-            v_bf = held.tile([P, P * PACK], BF16, name=f"v_bf{g}", tag=tag, align_bytes=64)
-            nc.scalar.copy(v_bf[:].bitcast(F32).rearrange("p (e u) -> p e u", u=2), turned[g][:].rearrange("p u e -> p e u"))
-            nc.vector.quantize_mx(v_codes[:, cols].bitcast(FP8X4), v_scales[:, cols], v_bf[:])
+        def quantize(name, width):
+            codes = held.tile([P, width], U32, name=f"{name}_codes", align_bytes=64)
+            scales = held.tile([P, width], U8, name=f"{name}_scales", align_bytes=64)
+            return codes, scales
 
+        v01_codes, v01_scales = quantize("v01", 2 * P)
         pick_and_turn(0)
-        pick_and_turn(1)
-        weave_and_quantize(0, "val_pool1")
-        pick_and_turn(2)
-        weave_and_quantize(1, "val_pool2")
+        for g in range(2):
+            pick_and_turn(g + 1)
+            v_bf = held.tile([P, I], BF16, name=f"v_bf{g}", tag=f"val_pool{g + 1}", align_bytes=64)
+            weave(g, v_bf[:])
+            cols = slice(g * P, (g + 1) * P)
+            nc.vector.quantize_mx(v01_codes[:, cols].bitcast(FP8X4), v01_scales[:, cols], v_bf[:])
 
         scores = psum.tile([P, PACK, Q], F32, name="scores", tag="turned1")
         for r in range(PACK):
             cols = slice(r * P, (r + 1) * P)
             nc.tensor.matmul_mx(scores[:, r, :], zk_codes[:, cols].bitcast(FP8X4), zk_scales[:, cols],
                                 q_codes[:].bitcast(FP8X4), q_scales[:], start=True, stop=True)
-        w_bf = held.tile([P, Q, PACK], BF16, name="w_bf", align_bytes=64)
-        nc.vector.scalar_tensor_tensor(
-            w_bf[:], scores[:].rearrange("p r q -> p q r"), 0.0,
-            factor[:].unsqueeze(1).to_broadcast([P, Q, PACK]), ALU.max, ALU.mult)
-        w_codes = held.tile([P, Q], U32, name="w_codes", align_bytes=64)
-        w_scales = held.tile([P, Q], U8, name="w_scales", align_bytes=64)
-        nc.vector.quantize_mx(w_codes[:].bitcast(FP8X4), w_scales[:], w_bf[:].rearrange("p q r -> p (q r)"))
 
-        weave_and_quantize(2, "v_bf2")
         pick_and_turn(3)
-        weave_and_quantize(3, "v_bf3")
+        wv2_bf = held.tile([P, 2, I], BF16, name="wv2_bf", tag="val_pool3", align_bytes=64)
+        nc.vector.scalar_tensor_tensor(
+            wv2_bf[:, 0, :].rearrange("p (q r) -> p q r", r=PACK), scores[:].rearrange("p r q -> p q r"), 0.0,
+            factor[:].unsqueeze(1).to_broadcast([P, Q, PACK]), ALU.max, ALU.mult)
+        weave(2, wv2_bf[:, 1, :])
+        wv2_codes, wv2_scales = quantize("wv2", 2 * P)
+        nc.vector.quantize_mx(wv2_codes[:].bitcast(FP8X4), wv2_scales[:], wv2_bf[:].rearrange("p j c -> p (j c)"))
+        v3_bf = held.tile([P, I], BF16, name="v3_bf", align_bytes=64)
+        weave(3, v3_bf[:])
+        v3_codes, v3_scales = quantize("v3", P)
+        nc.vector.quantize_mx(v3_codes[:].bitcast(FP8X4), v3_scales[:], v3_bf[:])
 
-        early = psum.tile([P, 3 * P], F32, name="early")
-        late = psum.tile([P, P], F32, name="late")
-        for acc, cols in ((early[:, 0 : 2 * P], slice(0, 2 * P)), (early[:, 2 * P : 3 * P], slice(2 * P, 3 * P)), (late[:], slice(3 * P, E))):
-            nc.tensor.matmul_mx(acc, w_codes[:].bitcast(FP8X4), w_scales[:],
-                                v_codes[:, cols].bitcast(FP8X4), v_scales[:, cols], start=True, stop=True)
-        for bank, cols in ((early, slice(0, 3 * P)), (late, slice(3 * P, E))):
-            result = held.tile([P, cols.stop - cols.start], F32, name=f"result{cols.start}")
-            nc.vector.tensor_copy(result[:], bank[:])
-            nc.sync.dma_start(out[:, cols], result[:])
+        early_acc = psum.tile([P, 3 * P], F32, name="early_acc")
+        late_acc = psum.tile([P, P], F32, name="late_acc")
+        for acc, codes, scales in (
+            (early_acc[:, 0 : 2 * P], v01_codes[:], v01_scales[:]),
+            (early_acc[:, 2 * P : 3 * P], wv2_codes[:, P : 2 * P], wv2_scales[:, P : 2 * P]),
+            (late_acc[:], v3_codes[:], v3_scales[:]),
+        ):
+            nc.tensor.matmul_mx(acc, wv2_codes[:, 0:P].bitcast(FP8X4), wv2_scales[:, 0:P], codes.bitcast(FP8X4), scales, start=True, stop=True)
+        early = held.tile([P, 3 * P], F32, name="early")
+        late = held.tile([P, P], F32, name="late")
+        nc.scalar.copy(early[:], early_acc[:])
+        nc.vector.tensor_copy(late[:], late_acc[:])
+        nc.sync.dma_start(out[:, 0 : 3 * P], early[:])
+        nc.sync.dma_start(out[:, 3 * P : E], late[:])

@@ -17,19 +17,21 @@ COPY = mybir.ActivationFunctionType.Copy
 
 P = 128
 PACK = 4
-LAST_THIRD_ON_VECTOR = 256
-LAST_VALUES_ON_VECTOR = 256
+LAST_THIRD_ON_VECTOR = 128
+LAST_VALUES_ON_VECTOR = 192
 
 
 def tile_attend_keymiddle_read_lean_kernel(tc, query, keys, slot_factor, vals, offs, offs2, offs3, out):
     nc = tc.nc
     with ExitStack() as ctx:
         held = ctx.enter_context(tc.tile_pool(name="held", bufs=1))
+        reused = ctx.enter_context(tc.tile_pool(name="reused", bufs=1))
         psum = ctx.enter_context(tc.psum_pool(name="psum", bufs=1))
 
         lists = [held.tile([P, I // 16], U16, name=f"list{n}") for n in range(3)]
         key_pool = [held.tile([P, T], F32, name=f"key_pool{t}") for t in range(PACK)]
-        val_pool = [held.tile([P, T], F32, name=f"val_pool{g}", align_bytes=64) for g in range(E // P)]
+        val_pool = [held.tile([P, T], F32, name=f"val_pool{g}", align_bytes=64) for g in range(E // P - 1)]
+        val_pool.append(reused.tile([P, T], F32, name="val_pool3", offset=0, align_bytes=64))
         q_raw = held.tile([P, PACK, Q], F32, name="q_raw")
         factor = held.tile([P, PACK], F32, name="factor")
         ident = held.tile([P, P], F32, name="ident")
@@ -77,26 +79,34 @@ def tile_attend_keymiddle_read_lean_kernel(tc, query, keys, slot_factor, vals, o
             nc.vector.tensor_tensor(capped[:, t, :], hi[:], third[:], ALU.min)
 
         zk_bf = held.tile([P, PACK, P, PACK], BF16, name="zk_bf", align_bytes=64)
-        nc.vector.tensor_tensor(
-            zk_bf[:].rearrange("p r s t -> p s t r"),
-            lo[:].rearrange("p t (s r) -> p s t r", r=PACK),
-            capped[:].rearrange("p t (s r) -> p s t r", r=PACK),
-            ALU.max,
-        )
         zk_codes = held.tile([P, I], U32, name="zk_codes", align_bytes=64)
         zk_scales = held.tile([P, I], U8, name="zk_scales", align_bytes=64)
-        nc.vector.quantize_mx(zk_codes[:].bitcast(FP8X4), zk_scales[:], zk_bf[:].rearrange("p r s t -> p (r s t)"))
+        halves = (slice(0, 2), slice(2, 4))
+        for rs in halves:
+            nc.vector.tensor_tensor(
+                zk_bf[:, rs].rearrange("p r s t -> p s t r"),
+                lo[:].rearrange("p t (s r) -> p s t r", r=PACK)[:, :, :, rs],
+                capped[:].rearrange("p t (s r) -> p s t r", r=PACK)[:, :, :, rs],
+                ALU.max,
+            )
+        for rs in halves:
+            cols = slice(rs.start * P, rs.stop * P)
+            nc.vector.quantize_mx(zk_codes[:, cols].bitcast(FP8X4), zk_scales[:, cols], zk_bf[:, rs].rearrange("p r s t -> p (r s t)"))
 
+        picks = []
         turned = []
 
-        def pick_and_turn(g):
+        def pick(g):
             picked = held.tile([P, I], BF16, name=f"picked{g}", align_bytes=64)
             shared = LAST_VALUES_ON_VECTOR if g == E // P - 1 else 0
             if shared:
                 on_vector(picked[:, 0:shared], val_pool[g], lists[0][:, 0 : shared // 16])
             on_scalar(picked[:, shared:I], val_pool[g], lists[0][:, shared // 16 : I // 16])
-            words = picked[:].bitcast(F32)
-            bank = psum.tile([P, 2, P], F32, name=f"turned{g}")
+            picks.append(picked)
+
+        def turn(g, tag):
+            words = picks[g][:].bitcast(F32)
+            bank = psum.tile([P, 2, P], F32, name=f"turned{g}", tag=tag)
             for u in range(2):
                 nc.tensor.transpose(bank[:, u, :], words[:, u : I // 2 : 2], ident[:])
             turned.append(bank)
@@ -109,42 +119,50 @@ def tile_attend_keymiddle_read_lean_kernel(tc, query, keys, slot_factor, vals, o
             scales = held.tile([P, width], U8, name=f"{name}_scales", align_bytes=64)
             return codes, scales
 
-        v01_codes, v01_scales = quantize("v01", 2 * P)
-        pick_and_turn(0)
         for g in range(2):
-            pick_and_turn(g + 1)
-            v_bf = held.tile([P, I], BF16, name=f"v_bf{g}", tag=f"val_pool{g + 1}", align_bytes=64)
-            weave(g, v_bf[:])
-            cols = slice(g * P, (g + 1) * P)
-            nc.vector.quantize_mx(v01_codes[:, cols].bitcast(FP8X4), v01_scales[:, cols], v_bf[:])
+            pick(g)
+            turn(g, f"turned{g}")
+        v0_bf = held.tile([P, I], BF16, name="v0_bf", tag="val_pool1", align_bytes=64)
+        weave(0, v0_bf[:])
+        v0_codes, v0_scales = quantize("v0", P)
+        nc.vector.quantize_mx(v0_codes[:].bitcast(FP8X4), v0_scales[:], v0_bf[:])
+        pick(2)
+        v1_bf = held.tile([P, I], BF16, name="v1_bf", tag="val_pool2", align_bytes=64)
+        weave(1, v1_bf[:])
 
-        scores = psum.tile([P, PACK, Q], F32, name="scores", tag="turned1")
+        scores = psum.tile([P, PACK, Q], F32, name="scores", tag="turned0")
         for r in range(PACK):
             cols = slice(r * P, (r + 1) * P)
             nc.tensor.matmul_mx(scores[:, r, :], zk_codes[:, cols].bitcast(FP8X4), zk_scales[:, cols],
                                 q_codes[:].bitcast(FP8X4), q_scales[:], start=True, stop=True)
-
-        pick_and_turn(3)
-        wv2_bf = held.tile([P, 2, I], BF16, name="wv2_bf", tag="val_pool3", align_bytes=64)
+        w_bf = held.tile([P, Q, PACK], BF16, name="w_bf", align_bytes=64)
         nc.vector.scalar_tensor_tensor(
-            wv2_bf[:, 0, :].rearrange("p (q r) -> p q r", r=PACK), scores[:].rearrange("p r q -> p q r"), 0.0,
+            w_bf[:], scores[:].rearrange("p r q -> p q r"), 0.0,
             factor[:].unsqueeze(1).to_broadcast([P, Q, PACK]), ALU.max, ALU.mult)
-        weave(2, wv2_bf[:, 1, :])
-        wv2_codes, wv2_scales = quantize("wv2", 2 * P)
-        nc.vector.quantize_mx(wv2_codes[:].bitcast(FP8X4), wv2_scales[:], wv2_bf[:].rearrange("p j c -> p (j c)"))
+
+        turn(2, "turned2")
+        pick(3)
+        turn(3, "turned3")
+        w_codes = reused.tile([P, Q], U32, name="w_codes", offset=0, align_bytes=64)
+        w_scales = held.tile([P, Q], U8, name="w_scales", align_bytes=64)
+        nc.vector.quantize_mx(w_codes[:].bitcast(FP8X4), w_scales[:], w_bf[:].rearrange("p q r -> p (q r)"))
+        v1_codes = reused.tile([P, P], U32, name="v1_codes", offset=512, align_bytes=64)
+        v1_scales = held.tile([P, P], U8, name="v1_scales", align_bytes=64)
+        nc.vector.quantize_mx(v1_codes[:].bitcast(FP8X4), v1_scales[:], v1_bf[:])
+        v2_bf = reused.tile([P, I], BF16, name="v2_bf", offset=1024, align_bytes=64)
         v3_bf = held.tile([P, I], BF16, name="v3_bf", align_bytes=64)
-        weave(3, v3_bf[:])
-        v3_codes, v3_scales = quantize("v3", P)
-        nc.vector.quantize_mx(v3_codes[:].bitcast(FP8X4), v3_scales[:], v3_bf[:])
+        operands = [(v0_codes[:], v0_scales[:]), (v1_codes[:], v1_scales[:])]
+        for g, v_bf in ((2, v2_bf), (3, v3_bf)):
+            weave(g, v_bf[:])
+            codes, scales = quantize(f"v{g}", P)
+            nc.vector.quantize_mx(codes[:].bitcast(FP8X4), scales[:], v_bf[:])
+            operands.append((codes[:], scales[:]))
 
         early_acc = psum.tile([P, 3 * P], F32, name="early_acc")
         late_acc = psum.tile([P, P], F32, name="late_acc")
-        for acc, codes, scales in (
-            (early_acc[:, 0 : 2 * P], v01_codes[:], v01_scales[:]),
-            (early_acc[:, 2 * P : 3 * P], wv2_codes[:, P : 2 * P], wv2_scales[:, P : 2 * P]),
-            (late_acc[:], v3_codes[:], v3_scales[:]),
-        ):
-            nc.tensor.matmul_mx(acc, wv2_codes[:, 0:P].bitcast(FP8X4), wv2_scales[:, 0:P], codes.bitcast(FP8X4), scales, start=True, stop=True)
+        for g, (codes, scales) in enumerate(operands):
+            acc = early_acc[:, g * P : (g + 1) * P] if g < 3 else late_acc[:]
+            nc.tensor.matmul_mx(acc, w_codes[:].bitcast(FP8X4), w_scales[:], codes.bitcast(FP8X4), scales, start=True, stop=True)
         early = held.tile([P, 3 * P], F32, name="early")
         late = held.tile([P, P], F32, name="late")
         nc.scalar.copy(early[:], early_acc[:])

from contextlib import ExitStack

import concourse.mybir as mybir
from concourse.masks import make_identity

D, T, I, Q, E = 512, 2048, 512, 128, 512
FLOPS = 2 * Q * I * D + 2 * Q * E * I

F32 = mybir.dt.float32
BF16 = mybir.dt.bfloat16
U32 = mybir.dt.uint32
U16 = mybir.dt.uint16
U8 = mybir.dt.uint8
FP8X4 = mybir.dt.float8_e4m3fn_x4
ALU = mybir.AluOpType
COPY = mybir.ActivationFunctionType.Copy

P = 128
PACK = 4
LAST_THIRD_ON_VECTOR = 128
LAST_VALUES_ON_VECTOR = 192


def tile_attend_keymiddle_read_lean_kernel(tc, query, keys, slot_factor, vals, offs, offs2, offs3, out):
    nc = tc.nc
    with ExitStack() as ctx:
        held = ctx.enter_context(tc.tile_pool(name="held", bufs=1))
        reused = ctx.enter_context(tc.tile_pool(name="reused", bufs=1))
        psum = ctx.enter_context(tc.psum_pool(name="psum", bufs=1))

        lists = [held.tile([P, I // 16], U16, name=f"list{n}") for n in range(3)]
        key_pool = [held.tile([P, T], F32, name=f"key_pool{t}") for t in range(PACK)]
        val_pool = [held.tile([P, T], F32, name=f"val_pool{g}", align_bytes=64) for g in range(E // P - 1)]
        val_pool.append(reused.tile([P, T], F32, name="val_pool3", offset=0, align_bytes=64))
        q_raw = held.tile([P, PACK, Q], F32, name="q_raw")
        factor = held.tile([P, PACK], F32, name="factor")
        ident = held.tile([P, P], F32, name="ident")

        keys_by_place = keys.rearrange("(p t) c -> p t c", t=PACK)
        nc.sync.dma_start(q_raw[:], query.rearrange("(p t) q -> p t q", t=PACK))
        nc.sync.dma_start(key_pool[0][:], keys_by_place[:, 0, :])
        for tile, src in zip(lists, (offs, offs2, offs3)):
            nc.sync.dma_start(tile[:], src)
        for t in range(1, PACK):
            nc.sync.dma_start(key_pool[t][:], keys_by_place[:, t, :])
        nc.sync.dma_start(factor[:], slot_factor.rearrange("o (p r) -> (o p) r", r=PACK))
        for g in range(E // P):
            nc.sync.dma_start(val_pool[g][:], vals[g * P : (g + 1) * P, :])
        make_identity(nc, ident[:])

        def on_vector(dst, window, offsets):
            nc.vector.tensor_copy(dst, window[:].indirect(offsets))

        def on_scalar(dst, window, offsets):
            nc.scalar.activation(dst, window[:].indirect(offsets), COPY)

        q_bf = held.tile([P, Q, PACK], BF16, name="q_bf", align_bytes=64)
        q_codes = held.tile([P, Q], U32, name="q_codes", align_bytes=64)
        q_scales = held.tile([P, Q], U8, name="q_scales", align_bytes=64)
        nc.scalar.activation(q_bf[:], q_raw[:].rearrange("p t q -> p q t"), COPY)
        nc.vector.quantize_mx(q_codes[:].bitcast(FP8X4), q_scales[:], q_bf[:].rearrange("p q t -> p (q t)"))

        lo = held.tile([P, PACK, I], F32, name="lo")
        capped = held.tile([P, PACK, I], F32, name="capped")
        for t in range(PACK):
            first = held.tile([P, I], F32, name=f"first{t}")
            second = held.tile([P, I], F32, name=f"second{t}")
            third = held.tile([P, I], F32, name=f"third{t}")
            hi = held.tile([P, I], F32, name=f"hi{t}")
            on_scalar(first[:], key_pool[t], lists[0][:])
            (on_vector if t < 2 else on_scalar)(second[:], key_pool[t], lists[1][:])
            shared = (0, 0, I, LAST_THIRD_ON_VECTOR)[t]
            if shared > 0:
                on_vector(third[:, 0:shared], key_pool[t], lists[2][:, 0 : shared // 16])
            if shared < I:
                on_scalar(third[:, shared:I], key_pool[t], lists[2][:, shared // 16 : I // 16])
            nc.vector.tensor_tensor(hi[:], first[:], second[:], ALU.max)
            nc.vector.tensor_tensor(lo[:, t, :], first[:], second[:], ALU.min)
            nc.vector.tensor_tensor(capped[:, t, :], hi[:], third[:], ALU.min)

        zk_bf = held.tile([P, PACK, P, PACK], BF16, name="zk_bf", align_bytes=64)
        zk_codes = held.tile([P, I], U32, name="zk_codes", align_bytes=64)
        zk_scales = held.tile([P, I], U8, name="zk_scales", align_bytes=64)
        halves = (slice(0, 2), slice(2, 4))
        for rs in halves:
            nc.vector.tensor_tensor(
                zk_bf[:, rs].rearrange("p r s t -> p s t r"),
                lo[:].rearrange("p t (s r) -> p s t r", r=PACK)[:, :, :, rs],
                capped[:].rearrange("p t (s r) -> p s t r", r=PACK)[:, :, :, rs],
                ALU.max,
            )
        for rs in halves:
            cols = slice(rs.start * P, rs.stop * P)
            nc.vector.quantize_mx(zk_codes[:, cols].bitcast(FP8X4), zk_scales[:, cols], zk_bf[:, rs].rearrange("p r s t -> p (r s t)"))

        picks = []
        turned = []

        def pick(g):
            picked = held.tile([P, I], BF16, name=f"picked{g}", align_bytes=64)
            shared = LAST_VALUES_ON_VECTOR if g == E // P - 1 else 0
            if shared:
                on_vector(picked[:, 0:shared], val_pool[g], lists[0][:, 0 : shared // 16])
            on_scalar(picked[:, shared:I], val_pool[g], lists[0][:, shared // 16 : I // 16])
            picks.append(picked)

        def turn(g, tag):
            words = picks[g][:].bitcast(F32)
            bank = psum.tile([P, 2, P], F32, name=f"turned{g}", tag=tag)
            for u in range(2):
                nc.tensor.transpose(bank[:, u, :], words[:, u : I // 2 : 2], ident[:])
            turned.append(bank)

        def weave(g, dst):
            nc.scalar.copy(dst.bitcast(F32).rearrange("p (e u) -> p e u", u=2), turned[g][:].rearrange("p u e -> p e u"))

        def quantize(name, width):
            codes = held.tile([P, width], U32, name=f"{name}_codes", align_bytes=64)
            scales = held.tile([P, width], U8, name=f"{name}_scales", align_bytes=64)
            return codes, scales

        for g in range(2):
            pick(g)
            turn(g, f"turned{g}")
        v0_bf = held.tile([P, I], BF16, name="v0_bf", tag="val_pool1", align_bytes=64)
        weave(0, v0_bf[:])
        v0_codes, v0_scales = quantize("v0", P)
        nc.vector.quantize_mx(v0_codes[:].bitcast(FP8X4), v0_scales[:], v0_bf[:])
        pick(2)
        v1_bf = held.tile([P, I], BF16, name="v1_bf", tag="val_pool2", align_bytes=64)
        weave(1, v1_bf[:])

        scores = psum.tile([P, PACK, Q], F32, name="scores", tag="turned0")
        for r in range(PACK):
            cols = slice(r * P, (r + 1) * P)
            nc.tensor.matmul_mx(scores[:, r, :], zk_codes[:, cols].bitcast(FP8X4), zk_scales[:, cols],
                                q_codes[:].bitcast(FP8X4), q_scales[:], start=True, stop=True)
        w_bf = held.tile([P, Q, PACK], BF16, name="w_bf", align_bytes=64)
        nc.vector.scalar_tensor_tensor(
            w_bf[:], scores[:].rearrange("p r q -> p q r"), 0.0,
            factor[:].unsqueeze(1).to_broadcast([P, Q, PACK]), ALU.max, ALU.mult)

        turn(2, "turned2")
        pick(3)
        turn(3, "turned3")
        w_codes = reused.tile([P, Q], U32, name="w_codes", offset=0, align_bytes=64)
        w_scales = held.tile([P, Q], U8, name="w_scales", align_bytes=64)
        nc.vector.quantize_mx(w_codes[:].bitcast(FP8X4), w_scales[:], w_bf[:].rearrange("p q r -> p (q r)"))
        v1_codes = reused.tile([P, P], U32, name="v1_codes", offset=512, align_bytes=64)
        v1_scales = held.tile([P, P], U8, name="v1_scales", align_bytes=64)
        nc.vector.quantize_mx(v1_codes[:].bitcast(FP8X4), v1_scales[:], v1_bf[:])
        v2_bf = reused.tile([P, I], BF16, name="v2_bf", offset=1024, align_bytes=64)
        v3_bf = held.tile([P, I], BF16, name="v3_bf", align_bytes=64)
        operands = [(v0_codes[:], v0_scales[:]), (v1_codes[:], v1_scales[:])]
        for g, v_bf in ((2, v2_bf), (3, v3_bf)):
            weave(g, v_bf[:])
            codes, scales = quantize(f"v{g}", P)
            nc.vector.quantize_mx(codes[:].bitcast(FP8X4), scales[:], v_bf[:])
            operands.append((codes[:], scales[:]))

        early_acc = psum.tile([P, 3 * P], F32, name="early_acc")
        late_acc = psum.tile([P, P], F32, name="late_acc")
        for g, (codes, scales) in enumerate(operands):
            acc = early_acc[:, g * P : (g + 1) * P] if g < 3 else late_acc[:]
            nc.tensor.matmul_mx(acc, w_codes[:].bitcast(FP8X4), w_scales[:], codes.bitcast(FP8X4), scales, start=True, stop=True)
        early = held.tile([P, 3 * P], F32, name="early")
        late = held.tile([P, P], F32, name="late")
        nc.scalar.copy(early[:], early_acc[:])
        nc.vector.tensor_copy(late[:], late_acc[:])
        nc.sync.dma_start(out[:, 0 : 3 * P], early[:])
        nc.sync.dma_start(out[:, 3 * P : E], late[:])
